import numpy as np
import ml_dtypes


def mxq(x, axis, fmt="e4m3"):
    dtype, down = {"e4m3": (ml_dtypes.float8_e4m3fn, 7), "e5m2": (ml_dtypes.float8_e5m2, 14)}[fmt]
    v = np.moveaxis(np.asarray(x, np.float32).astype(ml_dtypes.bfloat16).astype(np.float64), axis, -1)
    blocks = v.reshape(v.shape[:-1] + (-1, 32))
    amax = np.abs(blocks).max(-1, keepdims=True)
    byte = np.maximum(np.where(amax > 0, np.frexp(amax)[1] - 1 + 127, 0) - down, 1)
    scale = np.exp2(byte - 127.0)
    codes = (blocks / scale).astype(np.float32).astype(dtype).astype(np.float64)
    return np.moveaxis((codes * scale).reshape(v.shape), -1, axis)


WIDE = False


def mx_kscale(k):
    if not WIDE:
        return np.ones(k)
    levels = np.array([10, -10, 5, -5, 0])
    if k % 512:
        return np.exp2(np.random.permutation(np.resize(levels, k // 32))).repeat(32)
    a = np.empty((k // 512, 16))
    for p in range(k // 512):
        a[p, :8] = np.random.permutation(np.resize(levels, 8))
        for g in range(8):
            far = levels[np.abs(levels - a[p, g]) >= 10]
            a[p, g + 8] = far[np.random.randint(len(far))]
    return np.exp2(a.ravel()).repeat(32)


def f64(x):
    return np.asarray(x).astype(np.float64)


def striped(idx):
    return np.tile(idx.reshape(-1, 16).T, (8, 1)).astype(np.uint16)


def unstriped(offs):
    return offs[:16].T.reshape(-1).astype(np.int64)


def striped8(idx):
    return np.concatenate([x.reshape(-1, 16).T for x in idx]).astype(np.uint16)


def runs(offs, k):
    lists = np.stack([offs[16 * r : 16 * r + 16].T.reshape(-1) for r in range(8)]).astype(np.int64)
    return lists[np.arange(k) % 512 // 64]


def pack_weight(w):
    k, n = w.shape
    w = f64(np.asarray(w, np.float32).astype(ml_dtypes.bfloat16)).reshape(k // 32, 32, n)
    amax = np.abs(w).max(1)
    byte = np.clip(np.where(amax > 0, np.frexp(amax)[1] - 1 + 127 - 7, 1), 1, 254)
    scaled = (w * np.exp2(127.0 - byte)[:, None, :]).reshape(k, n).astype(np.float32)
    words = np.ascontiguousarray(scaled.reshape(k // 512, 128, 4, n).transpose(0, 1, 3, 2)).astype(ml_dtypes.float8_e4m3fn).view(np.uint8)
    return words, np.ascontiguousarray(byte.astype(np.uint8).reshape(k // 512, 16, n))


def unpack_weight(words, scales):
    g, p, n, _ = words.shape
    vals = np.ascontiguousarray(words).view(ml_dtypes.float8_e4m3fn).astype(np.float64) * np.repeat(np.exp2(scales.astype(np.float64) - 127.0), 8, axis=1)[..., None]
    return vals.transpose(0, 1, 3, 2).reshape(g * 512, n)


E2M1 = np.array([0.0, 0.5, 1.0, 1.5, 2.0, 3.0, 4.0, 6.0, -0.0, -0.5, -1.0, -1.5, -2.0, -3.0, -4.0, -6.0])


def pack_fp4(w):
    k, n = w.shape
    w = f64(np.asarray(w, np.float32).astype(ml_dtypes.bfloat16)).reshape(k // 32, 32, n)
    amax = np.abs(w).max(1)
    mant, ex = np.frexp(amax / 6.0)
    byte = np.clip(np.where(amax > 0, np.where(mant > 0.5, ex, ex - 1) + 127, 1), 1, 254)
    scaled = (w * np.exp2(127.0 - byte)[:, None, :]).reshape(k, n).astype(np.float32)
    c = np.ascontiguousarray(scaled.reshape(k // 512, 128, 4, n).transpose(0, 1, 3, 2)).astype(ml_dtypes.float4_e2m1fn).view(np.uint8) & 0xF
    words = (c[..., 0::2] | (c[..., 1::2] << 4)).reshape(k // 512, 128, 2 * n)
    return np.ascontiguousarray(words), np.ascontiguousarray(byte.astype(np.uint8).reshape(k // 512, 16, n))


def unpack_fp4(words, scales):
    g, _, n = scales.shape
    words = np.ascontiguousarray(words).reshape(g, 128, n, 2)
    nib = np.empty((g, 128, n, 4), np.uint8)
    nib[..., 0::2] = words & 0xF
    nib[..., 1::2] = words >> 4
    vals = E2M1[nib] * np.repeat(np.exp2(scales.astype(np.float64) - 127.0), 8, axis=1)[..., None]
    return vals.transpose(0, 1, 3, 2).reshape(g * 512, n)


def relu(v):
    return np.maximum(v, 0.0)

def planes(y):
    n, m = y.shape
    v = y.astype(np.float32).astype(ml_dtypes.bfloat16).astype(np.float64).reshape(n // 32, 32, m)
    top = np.abs(v).max(1)
    byte = np.clip(np.where(top > 0, np.frexp(top)[1] - 1 + 127 - 7, 1), 1, 254)
    codes = (v * np.exp2(127.0 - byte)[:, None, :]).reshape(n, m).astype(np.float32).astype(ml_dtypes.float8_e4m3fn).view(np.uint8)
    words = codes.reshape(n // 512, 128, 4, m).transpose(0, 1, 3, 2)
    return np.ascontiguousarray(words), np.ascontiguousarray(byte.astype(np.uint8).reshape(n // 512, 16, m))


K, T, S, H, J = 512, 2048, 512, 512, 512


def setup_inputs():
    n = np.random.standard_normal
    s = mx_kscale(K)[:, None]
    u = mx_kscale(S)
    packed_xT = pack_weight(n((K, T)) * s)
    packed_w1 = pack_fp4(n((K, H)) / np.sqrt(K) / s)
    return {
        "x_words": packed_xT[0],
        "x_scales": packed_xT[1],
        "w1_words": packed_w1[0],
        "w1_scales": packed_w1[1],
        "tab": n((H, J)).astype(np.float32),
        "ga": (np.random.uniform(0.5, 1.5, (H, 1)) * u[:, None]).astype(np.float32),
        "gb": (np.random.uniform(0.5, 1.5, (H, 1)) / u[:, None]).astype(np.float32),
        "offs": striped(np.random.permutation(T)[:S]),
        "n1": striped8(np.stack([np.random.permutation(S) for _ in range(8)])),
        "n2": striped8(np.stack([np.random.permutation(S) for _ in range(8)])),
        "n3": striped8(np.random.randint(0, J, (8, S))),
        "n4": striped8(np.stack([np.random.permutation(S) for _ in range(8)])),
        "n5": striped8(np.stack([np.random.permutation(S) for _ in range(8)])),
        "n6": striped8(np.stack([np.random.permutation(S) for _ in range(8)])),
        "n7": striped8(np.stack([np.random.permutation(S) for _ in range(8)])),
        "n8": striped8(np.stack([np.random.permutation(S) for _ in range(8)])),
    }


def reference(x_words, x_scales, w1_words, w1_scales, tab, ga, gb, offs, n1, n2, n3, n4, n5, n6, n7, n8):
    xq = unpack_weight(x_words, x_scales)[:, unstriped(offs)]
    y = unpack_fp4(w1_words, w1_scales).T @ xq
    pa = y - (y[np.arange(H)[:, None], runs(n1, H)])
    pb = y[np.arange(H)[:, None], runs(n2, H)] - y
    z = f64(ga) * (relu(np.minimum(pa, pb)) - (relu(-1.0 * np.maximum(pa, pb))))
    z2 = f64(gb) * (np.maximum(y + f64(tab)[np.arange(H)[:, None], runs(n3, H)], y[np.arange(H)[:, None], runs(n4, H)]))
    s = 0.0625 * ((mxq(z, 0, "e4m3").T @ mxq(z2, 0, "e4m3")))
    out_0 = 0.75 * ((s[np.arange(S)[:, None], runs(n5, S)]) * (s[np.arange(S)[:, None], runs(n6, S)]) - ((s[np.arange(S)[:, None], runs(n7, S)]) * (s[np.arange(S)[:, None], runs(n8, S)])))
    return (out_0,) + planes(out_0)

@@ -1,0 +1,230 @@
+import math
+from contextlib import ExitStack
+
+import concourse.mybir as mybir
+
+F32 = mybir.dt.float32
+BF16 = mybir.dt.bfloat16
+I32 = mybir.dt.int32
+U32 = mybir.dt.uint32
+U16 = mybir.dt.uint16
+U8 = mybir.dt.uint8
+FP8X4 = mybir.dt.float8_e4m3fn_x4
+FP4X4 = mybir.dt.float4_e2m1fn_x4
+ALU = mybir.AluOpType
+ACT = mybir.ActivationFunctionType
+
+P = 128
+R = 4
+T = 2048
+S = 512
+WIDE = 1024
+HEAD = 384
+FLOPS = 2 * 2 * 512 * 512 * 512
+
+
+def tile_picked_selfminmodkinddet_none_po_kernel(tc, x_words, x_scales, w1_words, w1_scales, tab, ga, gb, offs, n1, n2, n3, n4, n5, n6, n7, n8, out_0, out_1, out_2):
+    nc = tc.nc
+    with ExitStack() as ctx:
+        keep = ctx.enter_context(tc.tile_pool(name="keep", bufs=1))
+        psum = ctx.enter_context(tc.psum_pool(name="psum", bufs=1))
+
+        def sb(name, shape, dtype):
+            return keep.tile(shape, dtype, name=name, align_bytes=64)
+
+        def load_list(name, src):
+            tile = keep.tile([P, S // 16], U16, name=name)
+            nc.sync.dma_start(tile[:], src)
+            return tile
+
+        def load_scale_rows(tile, src, q):
+            nc.sync.dma_start(tile[32 * q : 32 * q + 4, :].bitcast(I32), src[0, 4 * q : 4 * q + 4, :].bitcast(I32))
+
+        xw = sb("xw", [P, T], I32)
+        xs = sb("xs", [P, T], U8)
+        ww = sb("ww", [P, 2 * S], U8)
+        ws = sb("ws", [P, S], U8)
+        nc.vector.memset(ws[:].bitcast(I32), 0)
+        nc.vector.memset(xs[:].bitcast(I32), 0)
+
+        l_offs = load_list("l_offs", offs)
+        nc.sync.dma_start(xw[:], x_words[0].rearrange("p c b -> p (c b)").bitcast(I32))
+        nc.sync.dma_start(ww[:].bitcast(I32), w1_words[0].bitcast(I32))
+        for q in range(4):
+            load_scale_rows(ws, w1_scales, q)
+        for q in range(4):
+            load_scale_rows(xs, x_scales, q)
+        tab_rows = tab.rearrange("(p t) c -> p t c", t=R)
+        tabw = [sb("tabw%d" % t, [P, WIDE], F32) for t in range(R)]
+        l3 = load_list("l3", n3)
+        nc.sync.dma_start(tabw[0][:, :S], tab_rows[:, 0, :])
+        l4 = load_list("l4", n4)
+        ga_sb = sb("ga_sb", [P, R], F32)
+        gb_sb = sb("gb_sb", [P, R], F32)
+        nc.sync.dma_start(gb_sb[:], gb.rearrange("(p t) o -> p (t o)", t=R))
+        nc.sync.dma_start(ga_sb[:], ga.rearrange("(p t) o -> p (t o)", t=R))
+        for t in range(1, R):
+            nc.sync.dma_start(tabw[t][:, :S], tab_rows[:, t, :])
+        l1 = load_list("l1", n1)
+        l2 = load_list("l2", n2)
+        l5 = load_list("l5", n5)
+        l6 = load_list("l6", n6)
+        l7 = load_list("l7", n7)
+        l8 = load_list("l8", n8)
+
+        wwd = sb("wwd", [P, 2 * S], U8)
+        wsd = sb("wsd", [P, S], U8)
+        nc.vector.tensor_copy(wwd[:].rearrange("p (t m b) -> p t m b", t=R, b=2), ww[:].rearrange("p (m t b) -> p t m b", t=R, b=2))
+        nc.vector.tensor_copy(wsd[:].rearrange("p (t m) -> p t m", t=R), ws[:].rearrange("p (m t) -> p t m", t=R))
+
+        xqw = sb("xqw", [P, S], U32)
+        xqs = sb("xqs", [P, S], U8)
+        nc.vector.tensor_copy(xqw[:], xw[:].bitcast(U32).indirect(l_offs[:]))
+        nc.vector.tensor_copy(xqs[:], xs[:].indirect(l_offs[:]))
+
+        ybank = [psum.tile([P, S], F32, name="ybank%d" % t) for t in range(R)]
+        for t in range(R):
+            nc.tensor.matmul_mx(
+                out=ybank[t][:],
+                lhsT=wwd[:, 2 * P * t : 2 * P * (t + 1)].bitcast(FP4X4),
+                lhsT_scale=wsd[:, P * t : P * (t + 1)],
+                rhs=xqw[:].bitcast(FP8X4),
+                rhs_scale=xqs[:],
+                start=True,
+                stop=True,
+            )
+
+        yw = [sb("yw%d" % t, [P, WIDE], F32) for t in range(R)]
+        for t in range(R):
+            nc.scalar.copy(yw[t][:, :S], ybank[t][:])
+        nga = sb("nga", [P, R], F32)
+        nc.scalar.activation(nga[:], ga_sb[:], ACT.Copy, scale=-1.0)
+        pos = [sb("pos%d" % t, [P, WIDE], F32) for t in range(R)]
+        neg = [sb("neg%d" % t, [P, WIDE], F32) for t in range(R)]
+
+        def scaled(t):
+            nc.scalar.activation(pos[t][:, :S], ybank[t][:], ACT.Copy, scale=ga_sb[:, t : t + 1])
+            nc.scalar.activation(neg[t][:, :S], ybank[t][:], ACT.Copy, scale=nga[:, t : t + 1])
+
+        u = [sb("u%d" % t, [P, S], F32) for t in range(R)]
+        v = [sb("v%d" % t, [P, S], F32) for t in range(R)]
+        m = [sb("m%d" % t, [P, S], F32) for t in range(R)]
+        z2b = sb("z2b", [P, S, R], BF16)
+
+        def finish_z2(t):
+            nc.vector.tensor_tensor(m[t][:], u[t][:], v[t][:], ALU.max)
+            nc.scalar.activation(z2b[:, :, t], m[t][:], ACT.Copy, scale=gb_sb[:, t : t + 1])
+
+        for t in range(R):
+            scaled(t)
+            nc.vector.tensor_copy(v[t][:], yw[t][:].indirect(l4[:]))
+            if t > 0:
+                finish_z2(t - 1)
+            nc.vector.tensor_tensor(u[t][:], tabw[t][:].indirect(l3[:]), yw[t][:, :S], ALU.add)
+
+        pa = [sb("pa%d" % t, [P, S], F32) for t in range(R)]
+        pb = [sb("pb%d" % t, [P, S], F32) for t in range(R)]
+        low = sb("low", [P, R, S], F32)
+        high = sb("high", [P, R, S], F32)
+        z2w = sb("z2w", [P, S], U32)
+        z2s = sb("z2s", [P, S], U8)
+
+        def by_place(ap):
+            return ap.rearrange("p (m d) -> p m d", d=R)
+
+        def dealt(ap):
+            return ap.rearrange("p (d m) -> p m d", d=R)
+
+        def clamp_low(t):
+            nc.vector.scalar_tensor_tensor(dealt(low[:, t, :]), by_place(pb[t][:]), 0.0, by_place(pa[t][:]), ALU.min, ALU.max)
+
+        for t in range(R):
+            nc.vector.tensor_tensor(pb[t][:], pos[t][:].indirect(l2[:]), neg[t][:, :S], ALU.add)
+            nc.scalar.activation(dealt(high[:, t, :]), by_place(pb[t][:]), ACT.Relu)
+            if t == 0:
+                finish_z2(R - 1)
+            else:
+                clamp_low(t - 1)
+            nc.vector.tensor_tensor(pa[t][:], neg[t][:].indirect(l1[:]), pos[t][:, :S], ALU.add)
+        nc.vector.quantize_mx(out=z2w[:].bitcast(FP8X4), scales=z2s[:], in_=z2b[:].rearrange("p c t -> p (c t)"))
+        clamp_low(R - 1)
+
+        zb = [sb("zb%d" % d, [P, P, R], BF16) for d in range(R)]
+        zw = [sb("zw%d" % d, [P, P], U32) for d in range(R)]
+        zs = [sb("zs%d" % d, [P, P], U8) for d in range(R)]
+        sbank = [psum.tile([P, S], F32, name="sbank%d" % d) for d in range(R)]
+        sw = [sb("sw%d" % d, [P, WIDE if d < R - 1 else S], F32) for d in range(R)]
+        s_scale = math.sqrt(0.75) / 16.0
+
+        def finish_z(d):
+            cols = slice(P * d, P * (d + 1))
+            nc.vector.tensor_tensor(
+                zb[d][:].rearrange("p (c i) t -> p c t i", i=4),
+                low[:, :, cols].rearrange("p t (c i) -> p c t i", i=4),
+                high[:, :, cols].rearrange("p t (c i) -> p c t i", i=4),
+                ALU.min,
+            )
+
+        def second_product(d):
+            nc.vector.quantize_mx(out=zw[d][:].bitcast(FP8X4), scales=zs[d][:], in_=zb[d][:].rearrange("p c t -> p (c t)"))
+            nc.tensor.matmul_mx(
+                out=sbank[d][:],
+                lhsT=zw[d][:].bitcast(FP8X4),
+                lhsT_scale=zs[d][:],
+                rhs=z2w[:].bitcast(FP8X4),
+                rhs_scale=z2s[:],
+                start=True,
+                stop=True,
+            )
+            nc.scalar.activation(sw[d][:, :S], sbank[d][:], ACT.Copy, scale=s_scale)
+
+        for d in range(R):
+            finish_z(d)
+            if d > 0:
+                second_product(d - 1)
+        second_product(R - 1)
+
+        out_rows = out_0.rearrange("(p t) c -> p t c", t=R)
+        o = sb("o", [P, R, S], F32)
+        ob_head = sb("ob_head", [P, HEAD, R], BF16)
+        ob_tail = sb("ob_tail", [P, S - HEAD, R], BF16)
+        ow = sb("ow", [P, S], U32)
+        osc = sb("osc", [P, S], U8)
+        words_out = out_1[0].rearrange("p c b -> p (c b)").bitcast(I32)
+        steps = [(d, 0, S) for d in range(R - 1)] + [(R - 1, 0, HEAD), (R - 1, HEAD, S)]
+        g5 = [sb("g5_%d" % k, [P, b - a], F32) for k, (d, a, b) in enumerate(steps)]
+        g7 = [sb("g7_%d" % k, [P, b - a], F32) for k, (d, a, b) in enumerate(steps)]
+        p1 = [sb("p1_%d" % k, [P, b - a], F32) for k, (d, a, b) in enumerate(steps)]
+        p2 = [sb("p2_%d" % k, [P, b - a], F32) for k, (d, a, b) in enumerate(steps)]
+
+        def finish_out(k):
+            d, a, b = steps[k]
+            nc.vector.tensor_tensor(o[:, d, a:b], p1[k][:], p2[k][:], ALU.subtract)
+            nc.sync.dma_start(out_rows[:, d, a:b], o[:, d, a:b])
+            if a == 0:
+                nc.scalar.copy(ob_head[:, :, d], o[:, d, :HEAD])
+
+        def planes(src, a, b):
+            nc.vector.quantize_mx(out=ow[:, a:b].bitcast(FP8X4), scales=osc[:, a:b], in_=src.rearrange("p c t -> p (c t)"))
+
+        for k, (d, a, b) in enumerate(steps):
+            part = slice(a // 16, b // 16)
+            nc.vector.tensor_copy(g5[k][:], sw[d][:].indirect(l5[:, part]))
+            if k > 0:
+                finish_out(k - 1)
+            nc.vector.tensor_copy(g7[k][:], sw[d][:].indirect(l7[:, part]))
+            nc.vector.tensor_tensor(p1[k][:], sw[d][:].indirect(l6[:, part]), g5[k][:], ALU.mult)
+            nc.vector.tensor_tensor(p2[k][:], sw[d][:].indirect(l8[:, part]), g7[k][:], ALU.mult)
+        finish_out(len(steps) - 1)
+        planes(ob_head[:, :256, :], 0, 256)
+        nc.vector.tensor_copy(
+            ob_tail[:].rearrange("p (c i) t -> p c t i", i=4),
+            o[:, :, HEAD:].rearrange("p t (c i) -> p c t i", i=4),
+        )
+        planes(ob_head[:, 256:, :], 256, HEAD)
+        nc.sync.dma_start(words_out[:, :HEAD], ow[:, :HEAD].bitcast(I32))
+        planes(ob_tail[:], HEAD, S)
+        nc.sync.dma_start(words_out[:, HEAD:], ow[:, HEAD:].bitcast(I32))
+        for q in range(4):
+            queue = nc.scalar if q % 2 == 0 else nc.sync
+            queue.dma_start(out_2[0, 4 * q : 4 * q + 4, :].bitcast(I32), osc[32 * q : 32 * q + 4, :].bitcast(I32))

@@ -2,6 +2,7 @@ import math
 from contextlib import ExitStack
 
 import concourse.mybir as mybir
+from concourse.masks import make_identity
 
 F32 = mybir.dt.float32
 BF16 = mybir.dt.bfloat16
@@ -32,6 +33,9 @@ def tile_picked_selfminmodkinddet_none_po_kernel(tc, x_words, x_scales, w1_words
         def sb(name, shape, dtype):
             return keep.tile(shape, dtype, name=name, align_bytes=64)
 
+        def bank(name, number):
+            return psum.tile([P, S], F32, name=name, tag="bank%d" % number)
+
         def load_list(name, src):
             tile = keep.tile([P, S // 16], U16, name=name)
             nc.sync.dma_start(tile[:], src)
@@ -40,92 +44,116 @@ def tile_picked_selfminmodkinddet_none_po_kernel(tc, x_words, x_scales, w1_words
         def load_scale_rows(tile, src, q):
             nc.sync.dma_start(tile[32 * q : 32 * q + 4, :].bitcast(I32), src[0, 4 * q : 4 * q + 4, :].bitcast(I32))
 
+        def block(k):
+            return slice(P * k, P * (k + 1))
+
         xw = sb("xw", [P, T], I32)
         xs = sb("xs", [P, T], U8)
         ww = sb("ww", [P, 2 * S], U8)
         ws = sb("ws", [P, S], U8)
-        nc.vector.memset(ws[:].bitcast(I32), 0)
         nc.vector.memset(xs[:].bitcast(I32), 0)
+        nc.vector.memset(ws[:].bitcast(I32), 0)
+        ident = sb("ident", [P, P], F32)
+        make_identity(nc, ident[:])
 
         l_offs = load_list("l_offs", offs)
-        nc.sync.dma_start(xw[:], x_words[0].rearrange("p c b -> p (c b)").bitcast(I32))
-        nc.sync.dma_start(ww[:].bitcast(I32), w1_words[0].bitcast(I32))
-        for q in range(4):
-            load_scale_rows(ws, w1_scales, q)
+        x_src = x_words[0].rearrange("p c b -> p (c b)").bitcast(I32)
+        nc.sync.dma_start(xw[:, : T // 4], x_src[:, : T // 4])
         for q in range(4):
             load_scale_rows(xs, x_scales, q)
+        nc.sync.dma_start(ww[:].bitcast(I32), w1_words[0].bitcast(I32))
+        nc.sync.dma_start(xw[:, T // 4 :], x_src[:, T // 4 :])
+        for q in range(4):
+            load_scale_rows(ws, w1_scales, q)
         tab_rows = tab.rearrange("(p t) c -> p t c", t=R)
         tabw = [sb("tabw%d" % t, [P, WIDE], F32) for t in range(R)]
-        l3 = load_list("l3", n3)
-        nc.sync.dma_start(tabw[0][:, :S], tab_rows[:, 0, :])
-        l4 = load_list("l4", n4)
         ga_sb = sb("ga_sb", [P, R], F32)
         gb_sb = sb("gb_sb", [P, R], F32)
+        l3 = load_list("l3", n3)
+        for t in range(R):
+            nc.sync.dma_start(tabw[t][:, :S], tab_rows[:, t, :])
         nc.sync.dma_start(gb_sb[:], gb.rearrange("(p t) o -> p (t o)", t=R))
         nc.sync.dma_start(ga_sb[:], ga.rearrange("(p t) o -> p (t o)", t=R))
-        for t in range(1, R):
-            nc.sync.dma_start(tabw[t][:, :S], tab_rows[:, t, :])
-        l1 = load_list("l1", n1)
+        l4 = load_list("l4", n4)
         l2 = load_list("l2", n2)
+        l1 = load_list("l1", n1)
         l5 = load_list("l5", n5)
-        l6 = load_list("l6", n6)
         l7 = load_list("l7", n7)
+        l6 = load_list("l6", n6)
         l8 = load_list("l8", n8)
 
-        wwd = sb("wwd", [P, 2 * S], U8)
-        wsd = sb("wsd", [P, S], U8)
-        nc.vector.tensor_copy(wwd[:].rearrange("p (t m b) -> p t m b", t=R, b=2), ww[:].rearrange("p (m t b) -> p t m b", t=R, b=2))
-        nc.vector.tensor_copy(wsd[:].rearrange("p (t m) -> p t m", t=R), ws[:].rearrange("p (m t) -> p t m", t=R))
-
+        wwd = [sb("wwd%d" % t, [P, 2 * P], U8) for t in range(R)]
+        wsd = [sb("wsd%d" % t, [P, P], U8) for t in range(R)]
         xqw = sb("xqw", [P, S], U32)
         xqs = sb("xqs", [P, S], U8)
-        nc.vector.tensor_copy(xqw[:], xw[:].bitcast(U32).indirect(l_offs[:]))
-        nc.vector.tensor_copy(xqs[:], xs[:].indirect(l_offs[:]))
+        ybank = [bank("ybank%d" % t, t) for t in range(R)]
 
-        ybank = [psum.tile([P, S], F32, name="ybank%d" % t) for t in range(R)]
-        for t in range(R):
+        def deal_words(t):
+            nc.vector.tensor_copy(wwd[t][:].rearrange("p (m b) -> p m b", b=2), ww[:].rearrange("p (m t b) -> p t m b", t=R, b=2)[:, t])
+
+        def first_product(t):
+            nc.vector.tensor_copy(wsd[t][:], ws[:].rearrange("p (m t) -> p t m", t=R)[:, t])
             nc.tensor.matmul_mx(
                 out=ybank[t][:],
-                lhsT=wwd[:, 2 * P * t : 2 * P * (t + 1)].bitcast(FP4X4),
-                lhsT_scale=wsd[:, P * t : P * (t + 1)],
+                lhsT=wwd[t][:].bitcast(FP4X4),
+                lhsT_scale=wsd[t][:],
                 rhs=xqw[:].bitcast(FP8X4),
                 rhs_scale=xqs[:],
                 start=True,
                 stop=True,
             )
 
+        nc.vector.tensor_copy(xqs[:], xs[:].indirect(l_offs[:]))
+        deal_words(0)
+        nc.vector.tensor_copy(xqw[:], xw[:].bitcast(U32).indirect(l_offs[:]))
+        first_product(0)
+        for t in range(1, R):
+            deal_words(t)
+            first_product(t)
+
         yw = [sb("yw%d" % t, [P, WIDE], F32) for t in range(R)]
+        u = [sb("u%d" % t, [P, S], F32) for t in range(R)]
         for t in range(R):
             nc.scalar.copy(yw[t][:, :S], ybank[t][:])
-        nga = sb("nga", [P, R], F32)
-        nc.scalar.activation(nga[:], ga_sb[:], ACT.Copy, scale=-1.0)
+            nc.vector.tensor_tensor(u[t][:], tabw[t][:].indirect(l3[:]), yw[t][:, :S], ALU.add)
+
+        gb_abs = sb("gb_abs", [P, R], F32)
+        gb_step = sb("gb_step", [P, R], F32)
+        ga_pos = sb("ga_pos", [P, R], F32)
+        ga_neg = sb("ga_neg", [P, R], F32)
+        nc.vector.tensor_scalar(gb_step[:], gb_sb[:], 0.0, 2.0, ALU.is_ge, ALU.mult)
+        nc.vector.scalar_tensor_tensor(ga_pos[:], gb_step[:], -1.0, ga_sb[:], ALU.add, ALU.mult)
+        nc.scalar.activation(ga_neg[:], ga_pos[:], ACT.Copy, scale=-1.0)
+        nc.scalar.activation(gb_abs[:], gb_sb[:], ACT.Abs)
+
         pos = [sb("pos%d" % t, [P, WIDE], F32) for t in range(R)]
         neg = [sb("neg%d" % t, [P, WIDE], F32) for t in range(R)]
+        for t in range(R):
+            nc.scalar.activation(pos[t][:, :S], ybank[t][:], ACT.Copy, scale=ga_pos[:, t : t + 1])
+            nc.scalar.activation(neg[t][:, :S], ybank[t][:], ACT.Copy, scale=ga_neg[:, t : t + 1])
 
-        def scaled(t):
-            nc.scalar.activation(pos[t][:, :S], ybank[t][:], ACT.Copy, scale=ga_sb[:, t : t + 1])
-            nc.scalar.activation(neg[t][:, :S], ybank[t][:], ACT.Copy, scale=nga[:, t : t + 1])
+        base = [sb("base%d" % t, [P, S], F32) for t in range(R)]
+        gap = [sb("gap%d" % t, [P, S], F32) for t in range(R)]
+        rise = [sb("rise%d" % t, [P, S], F32) for t in range(R)]
+        z2t_bank = [bank("z2t_bank%d" % k, R + k) for k in range(R)]
 
-        u = [sb("u%d" % t, [P, S], F32) for t in range(R)]
-        v = [sb("v%d" % t, [P, S], F32) for t in range(R)]
-        m = [sb("m%d" % t, [P, S], F32) for t in range(R)]
-        z2b = sb("z2b", [P, S, R], BF16)
-
-        def finish_z2(t):
-            nc.vector.tensor_tensor(m[t][:], u[t][:], v[t][:], ALU.max)
-            nc.scalar.activation(z2b[:, :, t], m[t][:], ACT.Copy, scale=gb_sb[:, t : t + 1])
+        def add_turned(out, first, second):
+            nc.tensor.matmul(out, lhsT=first, rhs=ident[:], start=True, stop=False, is_transpose=True)
+            nc.tensor.matmul(out, lhsT=second, rhs=ident[:], start=False, stop=True, is_transpose=True)
 
         for t in range(R):
-            scaled(t)
-            nc.vector.tensor_copy(v[t][:], yw[t][:].indirect(l4[:]))
-            if t > 0:
-                finish_z2(t - 1)
-            nc.vector.tensor_tensor(u[t][:], tabw[t][:].indirect(l3[:]), yw[t][:, :S], ALU.add)
+            nc.scalar.activation(base[t][:], u[t][:], ACT.Copy, scale=gb_abs[:, t : t + 1])
+        for t in range(R):
+            nc.vector.tensor_tensor(gap[t][:], yw[t][:].indirect(l4[:]), u[t][:], ALU.subtract)
+            nc.scalar.activation(rise[t][:], gap[t][:], ACT.Relu, scale=gb_abs[:, t : t + 1])
+            for k in range(R):
+                add_turned(z2t_bank[k][:, block(t)], base[t][:, block(k)], rise[t][:, block(k)])
 
         pa = [sb("pa%d" % t, [P, S], F32) for t in range(R)]
         pb = [sb("pb%d" % t, [P, S], F32) for t in range(R)]
         low = sb("low", [P, R, S], F32)
-        high = sb("high", [P, R, S], F32)
+        z2t = keep.tile([P, R * S], BF16, name="z2t", tag="shared", align_bytes=64)
+        z2b = sb("z2b", [P, S * R], BF16)
         z2w = sb("z2w", [P, S], U32)
         z2s = sb("z2s", [P, S], U8)
 
@@ -138,37 +166,52 @@ def tile_picked_selfminmodkinddet_none_po_kernel(tc, x_words, x_scales, w1_words
         def clamp_low(t):
             nc.vector.scalar_tensor_tensor(dealt(low[:, t, :]), by_place(pb[t][:]), 0.0, by_place(pa[t][:]), ALU.min, ALU.max)
 
+        def turn_z2_back():
+            for k in range(R):
+                nc.scalar.copy(
+                    z2t[:, S * k : S * (k + 1)].rearrange("j (h p e) -> j h p e", h=2, e=2),
+                    z2t_bank[k][:].rearrange("j (h e p) -> j h p e", h=2, e=2),
+                )
+            for half in range(2):
+                words = bank("z2_words%d" % half, R + half)
+                for k in range(2):
+                    for h in range(2):
+                        nc.tensor.transpose(words[:, block(2 * k + h)], z2t[:].bitcast(F32)[:, block(2 * (2 * half + k) + h)], ident[:])
+                nc.scalar.copy(
+                    z2b[:].bitcast(F32)[:, S * half : S * (half + 1)].rearrange("p (k j h) -> p k j h", k=2, h=2),
+                    words[:].rearrange("p (k h j) -> p k j h", k=2, h=2),
+                )
+
+        turn_z2_back()
+        high = keep.tile([P, R, S], F32, name="high", tag="shared", align_bytes=64)
         for t in range(R):
             nc.vector.tensor_tensor(pb[t][:], pos[t][:].indirect(l2[:]), neg[t][:, :S], ALU.add)
             nc.scalar.activation(dealt(high[:, t, :]), by_place(pb[t][:]), ACT.Relu)
-            if t == 0:
-                finish_z2(R - 1)
-            else:
+            if t > 0:
                 clamp_low(t - 1)
             nc.vector.tensor_tensor(pa[t][:], neg[t][:].indirect(l1[:]), pos[t][:, :S], ALU.add)
-        nc.vector.quantize_mx(out=z2w[:].bitcast(FP8X4), scales=z2s[:], in_=z2b[:].rearrange("p c t -> p (c t)"))
+        nc.vector.quantize_mx(out=z2w[:].bitcast(FP8X4), scales=z2s[:], in_=z2b[:])
         clamp_low(R - 1)
 
         zb = [sb("zb%d" % d, [P, P, R], BF16) for d in range(R)]
         zw = [sb("zw%d" % d, [P, P], U32) for d in range(R)]
         zs = [sb("zs%d" % d, [P, P], U8) for d in range(R)]
-        sbank = [psum.tile([P, S], F32, name="sbank%d" % d) for d in range(R)]
         sw = [sb("sw%d" % d, [P, WIDE if d < R - 1 else S], F32) for d in range(R)]
         s_scale = math.sqrt(0.75) / 16.0
 
         def finish_z(d):
-            cols = slice(P * d, P * (d + 1))
             nc.vector.tensor_tensor(
                 zb[d][:].rearrange("p (c i) t -> p c t i", i=4),
-                low[:, :, cols].rearrange("p t (c i) -> p c t i", i=4),
-                high[:, :, cols].rearrange("p t (c i) -> p c t i", i=4),
+                low[:, :, block(d)].rearrange("p t (c i) -> p c t i", i=4),
+                high[:, :, block(d)].rearrange("p t (c i) -> p c t i", i=4),
                 ALU.min,
             )
 
         def second_product(d):
             nc.vector.quantize_mx(out=zw[d][:].bitcast(FP8X4), scales=zs[d][:], in_=zb[d][:].rearrange("p c t -> p (c t)"))
+            sbank = bank("sbank%d" % d, d)
             nc.tensor.matmul_mx(
-                out=sbank[d][:],
+                out=sbank[:],
                 lhsT=zw[d][:].bitcast(FP8X4),
                 lhsT_scale=zs[d][:],
                 rhs=z2w[:].bitcast(FP8X4),
@@ -176,7 +219,7 @@ def tile_picked_selfminmodkinddet_none_po_kernel(tc, x_words, x_scales, w1_words
                 start=True,
                 stop=True,
             )
-            nc.scalar.activation(sw[d][:, :S], sbank[d][:], ACT.Copy, scale=s_scale)
+            nc.scalar.activation(sw[d][:, :S], sbank[:], ACT.Copy, scale=s_scale)
 
         for d in range(R):
             finish_z(d)
@@ -185,46 +228,85 @@ def tile_picked_selfminmodkinddet_none_po_kernel(tc, x_words, x_scales, w1_words
         second_product(R - 1)
 
         out_rows = out_0.rearrange("(p t) c -> p t c", t=R)
-        o = sb("o", [P, R, S], F32)
+        o_pair = [sb("o_pair%d" % h, [P, 2, S], F32) for h in range(2)]
+        o = [o_pair[d // 2][:, d % 2, :] for d in range(R)]
         ob_head = sb("ob_head", [P, HEAD, R], BF16)
         ob_tail = sb("ob_tail", [P, S - HEAD, R], BF16)
         ow = sb("ow", [P, S], U32)
         osc = sb("osc", [P, S], U8)
         words_out = out_1[0].rearrange("p c b -> p (c b)").bitcast(I32)
-        steps = [(d, 0, S) for d in range(R - 1)] + [(R - 1, 0, HEAD), (R - 1, HEAD, S)]
+        last = R - 1
+        steps = [(d, 0, S) for d in range(last)] + [(last, 0, 256), (last, 256, HEAD), (last, HEAD, S)]
         g5 = [sb("g5_%d" % k, [P, b - a], F32) for k, (d, a, b) in enumerate(steps)]
         g7 = [sb("g7_%d" % k, [P, b - a], F32) for k, (d, a, b) in enumerate(steps)]
         p1 = [sb("p1_%d" % k, [P, b - a], F32) for k, (d, a, b) in enumerate(steps)]
         p2 = [sb("p2_%d" % k, [P, b - a], F32) for k, (d, a, b) in enumerate(steps)]
 
-        def finish_out(k):
-            d, a, b = steps[k]
-            nc.vector.tensor_tensor(o[:, d, a:b], p1[k][:], p2[k][:], ALU.subtract)
-            nc.sync.dma_start(out_rows[:, d, a:b], o[:, d, a:b])
-            if a == 0:
-                nc.scalar.copy(ob_head[:, :, d], o[:, d, :HEAD])
+        def cast_pair(dst, h, a, b, first):
+            nc.scalar.copy(
+                dst[:, a - first : b - first, 2 * h : 2 * h + 2],
+                o_pair[h][:, :, a:b].rearrange("p e c -> p c e"),
+            )
+
+        def finish_on_tensor(d):
+            turned = bank("turned%d" % d, R + d % 2)
+            for k in range(R):
+                add_turned(turned[:, block(k)], p1[d][:, block(k)], p2[d][:, block(k)])
+            turned_sb = sb("turned_sb%d" % d, [P, S], F32)
+            nc.scalar.copy(turned_sb[:], turned[:])
+            back = bank("back%d" % d, R + (d + 1) % 2)
+            for k in range(R):
+                nc.tensor.transpose(back[:, block(k)], turned_sb[:, block(k)], ident[:])
+            nc.scalar.copy(o[d], back[:])
+            nc.scalar.dma_start(out_rows[:, d, :], o[d])
+            if d == 1:
+                cast_pair(ob_head, 0, 0, HEAD, 0)
+                cast_pair(ob_tail, 0, HEAD, S, HEAD)
 
         def planes(src, a, b):
             nc.vector.quantize_mx(out=ow[:, a:b].bitcast(FP8X4), scales=osc[:, a:b], in_=src.rearrange("p c t -> p (c t)"))
 
-        for k, (d, a, b) in enumerate(steps):
+        def fetch_first(k):
+            d, a, b = steps[k]
+            nc.vector.tensor_copy(g5[k][:], sw[d][:].indirect(l5[:, a // 16 : b // 16]))
+
+        def fetch_rest(k):
+            d, a, b = steps[k]
             part = slice(a // 16, b // 16)
-            nc.vector.tensor_copy(g5[k][:], sw[d][:].indirect(l5[:, part]))
-            if k > 0:
-                finish_out(k - 1)
-            nc.vector.tensor_copy(g7[k][:], sw[d][:].indirect(l7[:, part]))
+            if d < last:
+                nc.vector.tensor_scalar(g7[k][:], sw[d][:].indirect(l7[:, part]), -1.0, 0.0, ALU.mult, ALU.add)
+            else:
+                nc.vector.tensor_copy(g7[k][:], sw[d][:].indirect(l7[:, part]))
             nc.vector.tensor_tensor(p1[k][:], sw[d][:].indirect(l6[:, part]), g5[k][:], ALU.mult)
             nc.vector.tensor_tensor(p2[k][:], sw[d][:].indirect(l8[:, part]), g7[k][:], ALU.mult)
-        finish_out(len(steps) - 1)
+
+        def finish_on_vector(k):
+            d, a, b = steps[k]
+            nc.vector.tensor_tensor(o[d][:, a:b], p1[k][:], p2[k][:], ALU.subtract)
+            nc.sync.dma_start(out_rows[:, d, a:b], o[d][:, a:b])
+
+        for d in range(last):
+            fetch_first(d)
+            fetch_rest(d)
+            finish_on_tensor(d)
+        fetch_first(last)
+        fetch_rest(last)
+        fetch_first(last + 1)
+        finish_on_vector(last)
+        cast_pair(ob_head, 1, 0, 256, 0)
+        fetch_rest(last + 1)
+        nc.vector.tensor_copy(ob_tail[:, :, 2], o[2][:, HEAD:])
+        fetch_first(last + 2)
+        finish_on_vector(last + 1)
+        cast_pair(ob_head, 1, 256, HEAD, 0)
         planes(ob_head[:, :256, :], 0, 256)
-        nc.vector.tensor_copy(
-            ob_tail[:].rearrange("p (c i) t -> p c t i", i=4),
-            o[:, :, HEAD:].rearrange("p t (c i) -> p c t i", i=4),
-        )
+        nc.sync.dma_start(words_out[:, :256], ow[:, :256].bitcast(I32))
+        fetch_rest(last + 2)
         planes(ob_head[:, 256:, :], 256, HEAD)
-        nc.sync.dma_start(words_out[:, :HEAD], ow[:, :HEAD].bitcast(I32))
+        nc.vector.tensor_tensor(ob_tail[:, :, last], p1[last + 2][:], p2[last + 2][:], ALU.subtract)
+        finish_on_vector(last + 2)
         planes(ob_tail[:], HEAD, S)
-        nc.sync.dma_start(words_out[:, HEAD:], ow[:, HEAD:].bitcast(I32))
+        nc.scalar.dma_start(words_out[:, 256:], ow[:, 256:].bitcast(I32))
         for q in range(4):
             queue = nc.scalar if q % 2 == 0 else nc.sync
             queue.dma_start(out_2[0, 4 * q : 4 * q + 4, :].bitcast(I32), osc[32 * q : 32 * q + 4, :].bitcast(I32))

@@ -82,40 +82,40 @@ def tile_picked_selfminmodkinddet_none_po_kernel(tc, x_words, x_scales, w1_words
         l6 = load_list("l6", n6)
         l8 = load_list("l8", n8)
 
-        wwd = [sb("wwd%d" % t, [P, 2 * P], U8) for t in range(R)]
-        wsd = [sb("wsd%d" % t, [P, P], U8) for t in range(R)]
+        wwd = sb("wwd", [P, 2 * S], U8)
+        wsd = sb("wsd", [P, S], U8)
         xqw = sb("xqw", [P, S], U32)
         xqs = sb("xqs", [P, S], U8)
+        tab0 = sb("tab0", [P, S], F32)
         ybank = [bank("ybank%d" % t, t) for t in range(R)]
+        ws_by_tile = ws[:].rearrange("p (m t) -> p t m", t=R)
+        wsd_by_tile = wsd[:].rearrange("p (t m) -> p t m", t=R)
 
-        def deal_words(t):
-            nc.vector.tensor_copy(wwd[t][:].rearrange("p (m b) -> p m b", b=2), ww[:].rearrange("p (m t b) -> p t m b", t=R, b=2)[:, t])
-
-        def first_product(t):
-            nc.vector.tensor_copy(wsd[t][:], ws[:].rearrange("p (m t) -> p t m", t=R)[:, t])
+        nc.vector.tensor_copy(xqs[:], xs[:].indirect(l_offs[:]))
+        nc.vector.tensor_copy(wwd[:].rearrange("p (t m b) -> p t m b", t=R, b=2), ww[:].rearrange("p (m t b) -> p t m b", t=R, b=2))
+        nc.vector.tensor_copy(xqw[:], xw[:].bitcast(U32).indirect(l_offs[:]))
+        nc.vector.tensor_copy(wsd_by_tile[:, :1], ws_by_tile[:, :1])
+        nc.vector.tensor_copy(wsd_by_tile[:, 1:], ws_by_tile[:, 1:])
+        nc.vector.tensor_copy(tab0[:], tabw[0][:].indirect(l3[:]))
+        for t in range(R):
             nc.tensor.matmul_mx(
                 out=ybank[t][:],
-                lhsT=wwd[t][:].bitcast(FP4X4),
-                lhsT_scale=wsd[t][:],
+                lhsT=wwd[:, 2 * P * t : 2 * P * (t + 1)].bitcast(FP4X4),
+                lhsT_scale=wsd[:, block(t)],
                 rhs=xqw[:].bitcast(FP8X4),
                 rhs_scale=xqs[:],
                 start=True,
                 stop=True,
             )
 
-        nc.vector.tensor_copy(xqs[:], xs[:].indirect(l_offs[:]))
-        deal_words(0)
-        nc.vector.tensor_copy(xqw[:], xw[:].bitcast(U32).indirect(l_offs[:]))
-        first_product(0)
-        for t in range(1, R):
-            deal_words(t)
-            first_product(t)
-
         yw = [sb("yw%d" % t, [P, WIDE], F32) for t in range(R)]
         u = [sb("u%d" % t, [P, S], F32) for t in range(R)]
         for t in range(R):
             nc.scalar.copy(yw[t][:, :S], ybank[t][:])
-            nc.vector.tensor_tensor(u[t][:], tabw[t][:].indirect(l3[:]), yw[t][:, :S], ALU.add)
+            if t == 0:
+                nc.vector.tensor_tensor(u[t][:], tab0[:], yw[t][:, :S], ALU.add)
+            else:
+                nc.vector.tensor_tensor(u[t][:], tabw[t][:].indirect(l3[:]), yw[t][:, :S], ALU.add)
 
         gb_abs = sb("gb_abs", [P, R], F32)
         gb_step = sb("gb_step", [P, R], F32)
@@ -187,11 +187,11 @@ def tile_picked_selfminmodkinddet_none_po_kernel(tc, x_words, x_scales, w1_words
         for t in range(R):
             nc.vector.tensor_tensor(pb[t][:], pos[t][:].indirect(l2[:]), neg[t][:, :S], ALU.add)
             nc.scalar.activation(dealt(high[:, t, :]), by_place(pb[t][:]), ACT.Relu)
+            nc.vector.tensor_tensor(pa[t][:], neg[t][:].indirect(l1[:]), pos[t][:, :S], ALU.add)
             if t > 0:
                 clamp_low(t - 1)
-            nc.vector.tensor_tensor(pa[t][:], neg[t][:].indirect(l1[:]), pos[t][:, :S], ALU.add)
-        nc.vector.quantize_mx(out=z2w[:].bitcast(FP8X4), scales=z2s[:], in_=z2b[:])
         clamp_low(R - 1)
+        nc.vector.quantize_mx(out=z2w[:].bitcast(FP8X4), scales=z2s[:], in_=z2b[:])
 
         zb = [sb("zb%d" % d, [P, P, R], BF16) for d in range(R)]
         zw = [sb("zw%d" % d, [P, P], U32) for d in range(R)]
@@ -228,10 +228,8 @@ def tile_picked_selfminmodkinddet_none_po_kernel(tc, x_words, x_scales, w1_words
         second_product(R - 1)
 
         out_rows = out_0.rearrange("(p t) c -> p t c", t=R)
-        o_pair = [sb("o_pair%d" % h, [P, 2, S], F32) for h in range(2)]
-        o = [o_pair[d // 2][:, d % 2, :] for d in range(R)]
-        ob_head = sb("ob_head", [P, HEAD, R], BF16)
-        ob_tail = sb("ob_tail", [P, S - HEAD, R], BF16)
+        o_all = sb("o_all", [P, R, S], F32)
+        o = [o_all[:, d, :] for d in range(R)]
         ow = sb("ow", [P, S], U32)
         osc = sb("osc", [P, S], U8)
         words_out = out_1[0].rearrange("p c b -> p (c b)").bitcast(I32)
@@ -241,12 +239,6 @@ def tile_picked_selfminmodkinddet_none_po_kernel(tc, x_words, x_scales, w1_words
         g7 = [sb("g7_%d" % k, [P, b - a], F32) for k, (d, a, b) in enumerate(steps)]
         p1 = [sb("p1_%d" % k, [P, b - a], F32) for k, (d, a, b) in enumerate(steps)]
         p2 = [sb("p2_%d" % k, [P, b - a], F32) for k, (d, a, b) in enumerate(steps)]
-
-        def cast_pair(dst, h, a, b, first):
-            nc.scalar.copy(
-                dst[:, a - first : b - first, 2 * h : 2 * h + 2],
-                o_pair[h][:, :, a:b].rearrange("p e c -> p c e"),
-            )
 
         def finish_on_tensor(d):
             turned = bank("turned%d" % d, R + d % 2)
@@ -259,12 +251,16 @@ def tile_picked_selfminmodkinddet_none_po_kernel(tc, x_words, x_scales, w1_words
                 nc.tensor.transpose(back[:, block(k)], turned_sb[:, block(k)], ident[:])
             nc.scalar.copy(o[d], back[:])
             nc.scalar.dma_start(out_rows[:, d, :], o[d])
-            if d == 1:
-                cast_pair(ob_head, 0, 0, HEAD, 0)
-                cast_pair(ob_tail, 0, HEAD, S, HEAD)
 
-        def planes(src, a, b):
-            nc.vector.quantize_mx(out=ow[:, a:b].bitcast(FP8X4), scales=osc[:, a:b], in_=src.rearrange("p c t -> p (c t)"))
+        ob = [sb("ob%d" % k, [P, b - a, R], BF16) if d == last else None for k, (d, a, b) in enumerate(steps)]
+
+        def round_rows(copy, k):
+            d, a, b = steps[k]
+            copy(ob[k][:].rearrange("p (c i) t -> p c t i", i=4), o_all[:, :, a:b].rearrange("p t (c i) -> p c t i", i=4))
+
+        def planes(k):
+            d, a, b = steps[k]
+            nc.vector.quantize_mx(out=ow[:, a:b].bitcast(FP8X4), scales=osc[:, a:b], in_=ob[k][:].rearrange("p c t -> p (c t)"))
 
         def fetch_first(k):
             d, a, b = steps[k]
@@ -289,23 +285,18 @@ def tile_picked_selfminmodkinddet_none_po_kernel(tc, x_words, x_scales, w1_words
             fetch_first(d)
             fetch_rest(d)
             finish_on_tensor(d)
-        fetch_first(last)
-        fetch_rest(last)
-        fetch_first(last + 1)
-        finish_on_vector(last)
-        cast_pair(ob_head, 1, 0, 256, 0)
-        fetch_rest(last + 1)
-        nc.vector.tensor_copy(ob_tail[:, :, 2], o[2][:, HEAD:])
-        fetch_first(last + 2)
-        finish_on_vector(last + 1)
-        cast_pair(ob_head, 1, 256, HEAD, 0)
-        planes(ob_head[:, :256, :], 0, 256)
+        for k in range(last, last + 3):
+            fetch_first(k)
+            if k > last:
+                finish_on_vector(k - 1)
+                round_rows(nc.scalar.copy, k - 1)
+            fetch_rest(k)
+        planes(last)
         nc.sync.dma_start(words_out[:, :256], ow[:, :256].bitcast(I32))
-        fetch_rest(last + 2)
-        planes(ob_head[:, 256:, :], 256, HEAD)
-        nc.vector.tensor_tensor(ob_tail[:, :, last], p1[last + 2][:], p2[last + 2][:], ALU.subtract)
         finish_on_vector(last + 2)
-        planes(ob_tail[:], HEAD, S)
+        planes(last + 1)
+        round_rows(nc.vector.tensor_copy, last + 2)
+        planes(last + 2)
         nc.scalar.dma_start(words_out[:, 256:], ow[:, 256:].bitcast(I32))
         for q in range(4):
             queue = nc.scalar if q % 2 == 0 else nc.sync

import math
from contextlib import ExitStack

import concourse.mybir as mybir
from concourse.masks import make_identity

F32 = mybir.dt.float32
BF16 = mybir.dt.bfloat16
I32 = mybir.dt.int32
U32 = mybir.dt.uint32
U16 = mybir.dt.uint16
U8 = mybir.dt.uint8
FP8X4 = mybir.dt.float8_e4m3fn_x4
FP4X4 = mybir.dt.float4_e2m1fn_x4
ALU = mybir.AluOpType
ACT = mybir.ActivationFunctionType

P = 128
R = 4
T = 2048
S = 512
WIDE = 1024
HEAD = 384
FLOPS = 2 * 2 * 512 * 512 * 512


def tile_picked_selfminmodkinddet_none_po_kernel(tc, x_words, x_scales, w1_words, w1_scales, tab, ga, gb, offs, n1, n2, n3, n4, n5, n6, n7, n8, out_0, out_1, out_2):
    nc = tc.nc
    with ExitStack() as ctx:
        keep = ctx.enter_context(tc.tile_pool(name="keep", bufs=1))
        psum = ctx.enter_context(tc.psum_pool(name="psum", bufs=1))

        def sb(name, shape, dtype):
            return keep.tile(shape, dtype, name=name, align_bytes=64)

        def bank(name, number):
            return psum.tile([P, S], F32, name=name, tag="bank%d" % number)

        def load_list(name, src):
            tile = keep.tile([P, S // 16], U16, name=name)
            nc.sync.dma_start(tile[:], src)
            return tile

        def load_scale_rows(tile, src, q):
            nc.sync.dma_start(tile[32 * q : 32 * q + 4, :].bitcast(I32), src[0, 4 * q : 4 * q + 4, :].bitcast(I32))

        def block(k):
            return slice(P * k, P * (k + 1))

        xw = sb("xw", [P, T], I32)
        xs = sb("xs", [P, T], U8)
        ww = sb("ww", [P, 2 * S], U8)
        ws = sb("ws", [P, S], U8)
        nc.vector.memset(xs[:].bitcast(I32), 0)
        nc.vector.memset(ws[:].bitcast(I32), 0)
        ident = sb("ident", [P, P], F32)
        make_identity(nc, ident[:])

        l_offs = load_list("l_offs", offs)
        x_src = x_words[0].rearrange("p c b -> p (c b)").bitcast(I32)
        nc.sync.dma_start(xw[:, : T // 4], x_src[:, : T // 4])
        for q in range(4):
            load_scale_rows(xs, x_scales, q)
        nc.sync.dma_start(ww[:].bitcast(I32), w1_words[0].bitcast(I32))
        nc.sync.dma_start(xw[:, T // 4 :], x_src[:, T // 4 :])
        for q in range(4):
            load_scale_rows(ws, w1_scales, q)
        tab_rows = tab.rearrange("(p t) c -> p t c", t=R)
        tabw = [sb("tabw%d" % t, [P, WIDE], F32) for t in range(R)]
        ga_sb = sb("ga_sb", [P, R], F32)
        gb_sb = sb("gb_sb", [P, R], F32)
        l3 = load_list("l3", n3)
        for t in range(R):
            nc.sync.dma_start(tabw[t][:, :S], tab_rows[:, t, :])
        nc.sync.dma_start(gb_sb[:], gb.rearrange("(p t) o -> p (t o)", t=R))
        nc.sync.dma_start(ga_sb[:], ga.rearrange("(p t) o -> p (t o)", t=R))
        l4 = load_list("l4", n4)
        l2 = load_list("l2", n2)
        l1 = load_list("l1", n1)
        l5 = load_list("l5", n5)
        l7 = load_list("l7", n7)
        l6 = load_list("l6", n6)
        l8 = load_list("l8", n8)

        wwd = sb("wwd", [P, 2 * S], U8)
        wsd = sb("wsd", [P, S], U8)
        xqw = sb("xqw", [P, S], U32)
        xqs = sb("xqs", [P, S], U8)
        tab0 = sb("tab0", [P, S], F32)
        ybank = [bank("ybank%d" % t, t) for t in range(R)]
        ws_by_tile = ws[:].rearrange("p (m t) -> p t m", t=R)
        wsd_by_tile = wsd[:].rearrange("p (t m) -> p t m", t=R)

        nc.vector.tensor_copy(xqs[:], xs[:].indirect(l_offs[:]))
        nc.vector.tensor_copy(wwd[:].rearrange("p (t m b) -> p t m b", t=R, b=2), ww[:].rearrange("p (m t b) -> p t m b", t=R, b=2))
        nc.vector.tensor_copy(xqw[:], xw[:].bitcast(U32).indirect(l_offs[:]))
        nc.vector.tensor_copy(wsd_by_tile[:, :1], ws_by_tile[:, :1])
        nc.vector.tensor_copy(wsd_by_tile[:, 1:], ws_by_tile[:, 1:])
        nc.vector.tensor_copy(tab0[:], tabw[0][:].indirect(l3[:]))
        for t in range(R):
            nc.tensor.matmul_mx(
                out=ybank[t][:],
                lhsT=wwd[:, 2 * P * t : 2 * P * (t + 1)].bitcast(FP4X4),
                lhsT_scale=wsd[:, block(t)],
                rhs=xqw[:].bitcast(FP8X4),
                rhs_scale=xqs[:],
                start=True,
                stop=True,
            )

        yw = [sb("yw%d" % t, [P, WIDE], F32) for t in range(R)]
        u = [sb("u%d" % t, [P, S], F32) for t in range(R)]
        for t in range(R):
            nc.scalar.copy(yw[t][:, :S], ybank[t][:])
            if t == 0:
                nc.vector.tensor_tensor(u[t][:], tab0[:], yw[t][:, :S], ALU.add)
            else:
                nc.vector.tensor_tensor(u[t][:], tabw[t][:].indirect(l3[:]), yw[t][:, :S], ALU.add)

        gb_abs = sb("gb_abs", [P, R], F32)
        gb_step = sb("gb_step", [P, R], F32)
        ga_pos = sb("ga_pos", [P, R], F32)
        ga_neg = sb("ga_neg", [P, R], F32)
        nc.vector.tensor_scalar(gb_step[:], gb_sb[:], 0.0, 2.0, ALU.is_ge, ALU.mult)
        nc.vector.scalar_tensor_tensor(ga_pos[:], gb_step[:], -1.0, ga_sb[:], ALU.add, ALU.mult)
        nc.scalar.activation(ga_neg[:], ga_pos[:], ACT.Copy, scale=-1.0)
        nc.scalar.activation(gb_abs[:], gb_sb[:], ACT.Abs)

        pos = [sb("pos%d" % t, [P, WIDE], F32) for t in range(R)]
        neg = [sb("neg%d" % t, [P, WIDE], F32) for t in range(R)]
        for t in range(R):
            nc.scalar.activation(pos[t][:, :S], ybank[t][:], ACT.Copy, scale=ga_pos[:, t : t + 1])
            nc.scalar.activation(neg[t][:, :S], ybank[t][:], ACT.Copy, scale=ga_neg[:, t : t + 1])

        base = [sb("base%d" % t, [P, S], F32) for t in range(R)]
        gap = [sb("gap%d" % t, [P, S], F32) for t in range(R)]
        rise = [sb("rise%d" % t, [P, S], F32) for t in range(R)]
        z2t_bank = [bank("z2t_bank%d" % k, R + k) for k in range(R)]

        def add_turned(out, first, second):
            nc.tensor.matmul(out, lhsT=first, rhs=ident[:], start=True, stop=False, is_transpose=True)
            nc.tensor.matmul(out, lhsT=second, rhs=ident[:], start=False, stop=True, is_transpose=True)

        for t in range(R):
            nc.scalar.activation(base[t][:], u[t][:], ACT.Copy, scale=gb_abs[:, t : t + 1])
        for t in range(R):
            nc.vector.tensor_tensor(gap[t][:], yw[t][:].indirect(l4[:]), u[t][:], ALU.subtract)
            nc.scalar.activation(rise[t][:], gap[t][:], ACT.Relu, scale=gb_abs[:, t : t + 1])
            for k in range(R):
                add_turned(z2t_bank[k][:, block(t)], base[t][:, block(k)], rise[t][:, block(k)])

        pa = [sb("pa%d" % t, [P, S], F32) for t in range(R)]
        pb = [sb("pb%d" % t, [P, S], F32) for t in range(R)]
        low = sb("low", [P, R, S], F32)
        z2t = keep.tile([P, R * S], BF16, name="z2t", tag="shared", align_bytes=64)
        z2b = sb("z2b", [P, S * R], BF16)
        z2w = sb("z2w", [P, S], U32)
        z2s = sb("z2s", [P, S], U8)

        def by_place(ap):
            return ap.rearrange("p (m d) -> p m d", d=R)

        def dealt(ap):
            return ap.rearrange("p (d m) -> p m d", d=R)

        def clamp_low(t):
            nc.vector.scalar_tensor_tensor(dealt(low[:, t, :]), by_place(pb[t][:]), 0.0, by_place(pa[t][:]), ALU.min, ALU.max)

        def turn_z2_back():
            for k in range(R):
                nc.scalar.copy(
                    z2t[:, S * k : S * (k + 1)].rearrange("j (h p e) -> j h p e", h=2, e=2),
                    z2t_bank[k][:].rearrange("j (h e p) -> j h p e", h=2, e=2),
                )
            for half in range(2):
                words = bank("z2_words%d" % half, R + half)
                for k in range(2):
                    for h in range(2):
                        nc.tensor.transpose(words[:, block(2 * k + h)], z2t[:].bitcast(F32)[:, block(2 * (2 * half + k) + h)], ident[:])
                nc.scalar.copy(
                    z2b[:].bitcast(F32)[:, S * half : S * (half + 1)].rearrange("p (k j h) -> p k j h", k=2, h=2),
                    words[:].rearrange("p (k h j) -> p k j h", k=2, h=2),
                )

        turn_z2_back()
        high = keep.tile([P, R, S], F32, name="high", tag="shared", align_bytes=64)
        for t in range(R):
            nc.vector.tensor_tensor(pb[t][:], pos[t][:].indirect(l2[:]), neg[t][:, :S], ALU.add)
            nc.scalar.activation(dealt(high[:, t, :]), by_place(pb[t][:]), ACT.Relu)
            nc.vector.tensor_tensor(pa[t][:], neg[t][:].indirect(l1[:]), pos[t][:, :S], ALU.add)
            if t > 0:
                clamp_low(t - 1)
        clamp_low(R - 1)
        nc.vector.quantize_mx(out=z2w[:].bitcast(FP8X4), scales=z2s[:], in_=z2b[:])

        zb = [sb("zb%d" % d, [P, P, R], BF16) for d in range(R)]
        zw = [sb("zw%d" % d, [P, P], U32) for d in range(R)]
        zs = [sb("zs%d" % d, [P, P], U8) for d in range(R)]
        sw = [sb("sw%d" % d, [P, WIDE if d < R - 1 else S], F32) for d in range(R)]
        s_scale = math.sqrt(0.75) / 16.0

        def finish_z(d):
            nc.vector.tensor_tensor(
                zb[d][:].rearrange("p (c i) t -> p c t i", i=4),
                low[:, :, block(d)].rearrange("p t (c i) -> p c t i", i=4),
                high[:, :, block(d)].rearrange("p t (c i) -> p c t i", i=4),
                ALU.min,
            )

        def second_product(d):
            nc.vector.quantize_mx(out=zw[d][:].bitcast(FP8X4), scales=zs[d][:], in_=zb[d][:].rearrange("p c t -> p (c t)"))
            sbank = bank("sbank%d" % d, d)
            nc.tensor.matmul_mx(
                out=sbank[:],
                lhsT=zw[d][:].bitcast(FP8X4),
                lhsT_scale=zs[d][:],
                rhs=z2w[:].bitcast(FP8X4),
                rhs_scale=z2s[:],
                start=True,
                stop=True,
            )
            nc.scalar.activation(sw[d][:, :S], sbank[:], ACT.Copy, scale=s_scale)

        for d in range(R):
            finish_z(d)
            if d > 0:
                second_product(d - 1)
        second_product(R - 1)

        out_rows = out_0.rearrange("(p t) c -> p t c", t=R)
        o_all = sb("o_all", [P, R, S], F32)
        o = [o_all[:, d, :] for d in range(R)]
        ow = sb("ow", [P, S], U32)
        osc = sb("osc", [P, S], U8)
        words_out = out_1[0].rearrange("p c b -> p (c b)").bitcast(I32)
        last = R - 1
        steps = [(d, 0, S) for d in range(last)] + [(last, 0, 256), (last, 256, HEAD), (last, HEAD, S)]
        g5 = [sb("g5_%d" % k, [P, b - a], F32) for k, (d, a, b) in enumerate(steps)]
        g7 = [sb("g7_%d" % k, [P, b - a], F32) for k, (d, a, b) in enumerate(steps)]
        p1 = [sb("p1_%d" % k, [P, b - a], F32) for k, (d, a, b) in enumerate(steps)]
        p2 = [sb("p2_%d" % k, [P, b - a], F32) for k, (d, a, b) in enumerate(steps)]

        def finish_on_tensor(d):
            turned = bank("turned%d" % d, R + d % 2)
            for k in range(R):
                add_turned(turned[:, block(k)], p1[d][:, block(k)], p2[d][:, block(k)])
            turned_sb = sb("turned_sb%d" % d, [P, S], F32)
            nc.scalar.copy(turned_sb[:], turned[:])
            back = bank("back%d" % d, R + (d + 1) % 2)
            for k in range(R):
                nc.tensor.transpose(back[:, block(k)], turned_sb[:, block(k)], ident[:])
            nc.scalar.copy(o[d], back[:])
            nc.scalar.dma_start(out_rows[:, d, :], o[d])

        ob = [sb("ob%d" % k, [P, b - a, R], BF16) if d == last else None for k, (d, a, b) in enumerate(steps)]

        def round_rows(copy, k):
            d, a, b = steps[k]
            copy(ob[k][:].rearrange("p (c i) t -> p c t i", i=4), o_all[:, :, a:b].rearrange("p t (c i) -> p c t i", i=4))

        def planes(k):
            d, a, b = steps[k]
            nc.vector.quantize_mx(out=ow[:, a:b].bitcast(FP8X4), scales=osc[:, a:b], in_=ob[k][:].rearrange("p c t -> p (c t)"))

        def fetch_first(k):
            d, a, b = steps[k]
            nc.vector.tensor_copy(g5[k][:], sw[d][:].indirect(l5[:, a // 16 : b // 16]))

        def fetch_rest(k):
            d, a, b = steps[k]
            part = slice(a // 16, b // 16)
            if d < last:
                nc.vector.tensor_scalar(g7[k][:], sw[d][:].indirect(l7[:, part]), -1.0, 0.0, ALU.mult, ALU.add)
            else:
                nc.vector.tensor_copy(g7[k][:], sw[d][:].indirect(l7[:, part]))
            nc.vector.tensor_tensor(p1[k][:], sw[d][:].indirect(l6[:, part]), g5[k][:], ALU.mult)
            nc.vector.tensor_tensor(p2[k][:], sw[d][:].indirect(l8[:, part]), g7[k][:], ALU.mult)

        def finish_on_vector(k):
            d, a, b = steps[k]
            nc.vector.tensor_tensor(o[d][:, a:b], p1[k][:], p2[k][:], ALU.subtract)
            nc.sync.dma_start(out_rows[:, d, a:b], o[d][:, a:b])

        for d in range(last):
            fetch_first(d)
            fetch_rest(d)
            finish_on_tensor(d)
        for k in range(last, last + 3):
            fetch_first(k)
            if k > last:
                finish_on_vector(k - 1)
                round_rows(nc.scalar.copy, k - 1)
            fetch_rest(k)
        planes(last)
        nc.sync.dma_start(words_out[:, :256], ow[:, :256].bitcast(I32))
        finish_on_vector(last + 2)
        planes(last + 1)
        round_rows(nc.vector.tensor_copy, last + 2)
        planes(last + 2)
        nc.scalar.dma_start(words_out[:, 256:], ow[:, 256:].bitcast(I32))
        for q in range(4):
            queue = nc.scalar if q % 2 == 0 else nc.sync
            queue.dma_start(out_2[0, 4 * q : 4 * q + 4, :].bitcast(I32), osc[32 * q : 32 * q + 4, :].bitcast(I32))
